import numpy as np
import ml_dtypes


def mxq(x, axis, fmt="e4m3"):
    dtype, down = {"e4m3": (ml_dtypes.float8_e4m3fn, 7), "e5m2": (ml_dtypes.float8_e5m2, 14)}[fmt]
    v = np.moveaxis(np.asarray(x, np.float32).astype(ml_dtypes.bfloat16).astype(np.float64), axis, -1)
    blocks = v.reshape(v.shape[:-1] + (-1, 32))
    amax = np.abs(blocks).max(-1, keepdims=True)
    byte = np.maximum(np.where(amax > 0, np.frexp(amax)[1] - 1 + 127, 0) - down, 1)
    scale = np.exp2(byte - 127.0)
    codes = (blocks / scale).astype(np.float32).astype(dtype).astype(np.float64)
    return np.moveaxis((codes * scale).reshape(v.shape), -1, axis)


WIDE = False


def mx_kscale(k):
    if not WIDE:
        return np.ones(k)
    levels = np.array([10, -10, 5, -5, 0])
    if k % 512:
        return np.exp2(np.random.permutation(np.resize(levels, k // 32))).repeat(32)
    a = np.empty((k // 512, 16))
    for p in range(k // 512):
        a[p, :8] = np.random.permutation(np.resize(levels, 8))
        for g in range(8):
            far = levels[np.abs(levels - a[p, g]) >= 10]
            a[p, g + 8] = far[np.random.randint(len(far))]
    return np.exp2(a.ravel()).repeat(32)


def f64(x):
    return np.asarray(x).astype(np.float64)


def striped(idx):
    return np.tile(idx.reshape(-1, 16).T, (8, 1)).astype(np.uint16)


def unstriped(offs):
    return offs[:16].T.reshape(-1).astype(np.int64)


E2M1 = np.array([0.0, 0.5, 1.0, 1.5, 2.0, 3.0, 4.0, 6.0, -0.0, -0.5, -1.0, -1.5, -2.0, -3.0, -4.0, -6.0])


def pack_weight(w, fmt):
    k, n = w.shape
    w = f64(np.asarray(w, np.float32).astype(ml_dtypes.bfloat16)).reshape(k // 32, 32, n)
    amax = np.abs(w).max(1)
    if fmt == "e4m3":
        byte = np.frexp(amax)[1] - 1 + 127 - 7
    else:
        mant, ex = np.frexp(amax / 6.0)
        byte = np.where(mant > 0.5, ex, ex - 1) + 127
    byte = np.clip(np.where(amax > 0, byte, 1), 1, 254)
    scaled = (w * np.exp2(127.0 - byte)[:, None, :]).reshape(k, n).astype(np.float32)
    by_word = np.ascontiguousarray(scaled.reshape(k // 512, 128, 4, n).transpose(0, 1, 3, 2))
    if fmt == "e4m3":
        words = by_word.astype(ml_dtypes.float8_e4m3fn).view(np.uint8)
    else:
        c = by_word.astype(ml_dtypes.float4_e2m1fn).view(np.uint8) & 0xF
        words = (c[..., 0::2] | (c[..., 1::2] << 4)).reshape(k // 512, 128, 2 * n)
    return np.ascontiguousarray(words), np.ascontiguousarray(byte.astype(np.uint8).reshape(k // 512, 16, n))


def unpack_weight(words, scales, fmt):
    g, _, n = scales.shape
    words = np.ascontiguousarray(words).reshape(g, 128, n, -1)
    if fmt == "e4m3":
        vals = words.view(ml_dtypes.float8_e4m3fn).astype(np.float64)
    else:
        nib = np.empty((g, 128, n, 4), np.uint8)
        nib[..., 0::2] = words & 0xF
        nib[..., 1::2] = words >> 4
        vals = E2M1[nib]
    vals = vals * np.repeat(np.exp2(scales.astype(np.float64) - 127.0), 8, axis=1)[..., None]
    return vals.transpose(0, 1, 3, 2).reshape(g * 512, n)


def gelu(v):
    return 0.5 * v * (1.0 + np.tanh(np.sqrt(2.0 / np.pi) * (v + 0.044715 * v**3)))


def bf(x):
    return np.asarray(x, np.float32).astype(ml_dtypes.bfloat16)

def planes(Y):
    n, m = Y.shape
    b = f64(bf(Y)).reshape(n // 32, 32, m)
    amax = np.abs(b).max(1)
    byte = np.clip(np.where(amax > 0, np.frexp(amax)[1] - 1 + 127 - 7, 1), 1, 254)
    codes = (b * np.exp2(127.0 - byte)[:, None, :]).reshape(n, m).astype(np.float32).astype(ml_dtypes.float8_e4m3fn).view(np.uint8)
    words = codes.reshape(n // 512, 128, 4, m).transpose(0, 1, 3, 2)
    return np.ascontiguousarray(words), np.ascontiguousarray(byte.astype(np.uint8).reshape(n // 512, 16, m))


K, H, T, S = 1024, 1536, 2048, 512


def setup_inputs():
    n = np.random.standard_normal
    s = mx_kscale(K)[:, None]
    u = mx_kscale(H)[:, None]
    e = np.exp(0.8 * n(K))[:, None]
    e = e / np.sqrt(np.mean(e * e))
    w = 0.8 * e * n((K, H)) / np.sqrt(K)
    tab_words, tab_scales = pack_weight(n((K, T)) * s, "e4m3")
    wt_words, wt_scales = pack_weight(w.T / u, "e2m1")
    return {
        "tab_words": tab_words,
        "tab_scales": tab_scales,
        "offs": striped(np.random.permutation(T)[:S]),
        "w1": (w / s).astype(np.float32),
        "gT": (2.0 * n((H, T))).astype(np.float32),
        "gain": (np.exp(0.3 * n(H)) * u[:, 0]).astype(np.float32),
        "wt_words": wt_words,
        "wt_scales": wt_scales,
    }


def reference(tab_words, tab_scales, offs, w1, gT, gain, wt_words, wt_scales):
    v = unpack_weight(tab_words, tab_scales, "e4m3")[:, unstriped(offs)]
    g = f64(gT)[:, unstriped(offs)]
    a = mxq(f64(w1), 0, "e4m3").T @ v
    h = np.tanh(a)
    delta = (1.0 - h * h) * g * f64(gain)[:, None]
    wt = unpack_weight(wt_words, wt_scales, "e2m1")
    y = wt.T @ mxq(delta, 0, "e4m3")
    words, scales = planes(y)
    return y, words, scales

@@ -1,0 +1,253 @@
+from contextlib import ExitStack
+
+import concourse.mybir as mybir
+
+K, H, T, S = 1024, 1536, 2048, 512
+FLOPS = 2 * K * H * S * 2
+
+F32 = mybir.dt.float32
+BF16 = mybir.dt.bfloat16
+I32 = mybir.dt.int32
+U32 = mybir.dt.uint32
+U16 = mybir.dt.uint16
+U8 = mybir.dt.uint8
+FP8X4 = mybir.dt.float8_e4m3fn_x4
+FP4X4 = mybir.dt.float4_e2m1fn_x4
+ACT = mybir.ActivationFunctionType
+ALU = mybir.AluOpType
+
+P = 128
+PACK = 4
+PASS = P * PACK
+K_PASSES = K // PASS
+R_PASSES = H // PASS
+HALF = S // 2
+TAB_PLANE = 8
+G_BUFS = 6
+
+
+def tile_list_recomputed_tanh_backprop_kernel(
+    tc, tab_words, tab_scales, offs, w1, gT, gain, wt_words, wt_scales, out_0, out_1, out_2
+):
+    nc = tc.nc
+    with ExitStack() as ctx:
+        keep = ctx.enter_context(tc.tile_pool(name="keep", bufs=1))
+        big = ctx.enter_context(tc.tile_pool(name="big", bufs=2))
+        stage = ctx.enter_context(tc.tile_pool(name="stage", bufs=4))
+        rows = ctx.enter_context(tc.tile_pool(name="rows", bufs=G_BUFS))
+        psum = ctx.enter_context(tc.psum_pool(name="psum", bufs=1))
+
+        offsets = keep.tile([P, S // 16], U16, name="offsets")
+        wt_raw = keep.tile([P, R_PASSES, 2 * K], U8, name="wt_raw")
+        wt_raw_scales = keep.tile([P, R_PASSES, K], U8, name="wt_raw_scales")
+        tab_raw_scales = keep.tile([P, T], U8, name="tab_raw_scales")
+        gain_sb = keep.tile([P, R_PASSES, PACK], F32, name="gain_sb")
+        neg_gain = keep.tile([P, R_PASSES, PACK], F32, name="neg_gain")
+
+        nc.vector.memset(wt_raw_scales[:].bitcast(I32), 0)
+        nc.vector.memset(tab_raw_scales[:].bitcast(I32), 0)
+
+        nc.sync.dma_start(wt_raw[:].bitcast(I32), wt_words.rearrange("a p c -> p a c").bitcast(I32))
+        for q in range(4):
+            nc.sync.dma_start(
+                wt_raw_scales[32 * q : 32 * q + 4, :, :].bitcast(I32),
+                wt_scales[:, 4 * q : 4 * q + 4, :].rearrange("a r c -> r a c").bitcast(I32),
+            )
+        nc.sync.dma_start(offsets[:], offs)
+        w1_raw = []
+        for a in range(K_PASSES):
+            raw = big.tile([P, PACK, H], F32, name="w1_raw", tag="big")
+            nc.sync.dma_start(raw[:], w1[PASS * a : PASS * (a + 1), :].rearrange("(p j) r -> p j r", j=PACK))
+            w1_raw.append(raw)
+        nc.sync.dma_start(gain_sb[:], gain.rearrange("(b p t) -> p b t", p=P, t=PACK))
+        for q in range(4):
+            nc.sync.dma_start(
+                tab_raw_scales[32 * q + TAB_PLANE : 32 * q + TAB_PLANE + 4 * K_PASSES, :].bitcast(I32),
+                tab_scales[:, 4 * q : 4 * q + 4, :].bitcast(I32),
+            )
+        tab_raw = []
+        for a in range(K_PASSES):
+            raw = keep.tile([P, T], I32, name="tab_raw%d" % a)
+            nc.sync.dma_start(raw[:], tab_words[a].rearrange("p t i -> p (t i)").bitcast(I32))
+            tab_raw.append(raw)
+
+        wt_codes = keep.tile([P, R_PASSES, 2 * K], U8, name="wt_codes", align_bytes=64)
+        wt_plane = keep.tile([P, R_PASSES, K], U8, name="wt_plane", align_bytes=64)
+        for b in range(R_PASSES):
+            nc.vector.tensor_copy(
+                wt_codes[:, b, :].bitcast(U16).rearrange("p (g t q) -> p g t q", t=PACK, q=P),
+                wt_raw[:, b, :].bitcast(U16).rearrange("p (g q t) -> p g t q", t=PACK, q=P),
+            )
+        for b in range(R_PASSES):
+            nc.vector.tensor_copy(
+                wt_plane[:, b, :].rearrange("p (g t q) -> p g t q", t=PACK, q=P),
+                wt_raw_scales[:, b, :].rearrange("p (g q t) -> p g t q", t=PACK, q=P),
+            )
+        nc.vector.tensor_scalar(neg_gain[:], gain_sb[:], -1.0, None, ALU.mult)
+
+        w1_codes = keep.tile([P, K_PASSES, H], U32, name="w1_codes", align_bytes=64)
+        w1_plane = keep.tile([P, K_PASSES, H], U8, name="w1_plane", align_bytes=64)
+        v_codes = keep.tile([P, K_PASSES, S], U32, name="v_codes", align_bytes=64)
+        v_plane = keep.tile([P, S], U8, name="v_plane", align_bytes=64)
+
+        def round_w1(a, b, on_scalar):
+            grouped = stage.tile([P, PASS * PACK], BF16, name="grouped", tag="stage", align_bytes=64)
+            dst = grouped[:].rearrange("p (t m j) -> p m t j", t=PACK, j=PACK)
+            src = w1_raw[a][:, :, PASS * b : PASS * (b + 1)].rearrange("p j (m t) -> p m t j", t=PACK)
+            if on_scalar:
+                nc.scalar.copy(dst, src)
+            else:
+                nc.vector.tensor_copy(dst, src)
+            return grouped
+
+        def quantise_w1(a, b, grouped):
+            cols = slice(PASS * b, PASS * (b + 1))
+            nc.vector.quantize_mx(w1_codes[:, a, cols].bitcast(FP8X4), w1_plane[:, a, cols], grouped[:])
+
+        first = [round_w1(0, b, b == 0) for b in range(R_PASSES)]
+        nc.vector.tensor_copy(v_plane[:], tab_raw_scales[:].indirect(offsets[:]))
+        for b in (1, 2, 0):
+            quantise_w1(0, b, first[b])
+        second = [round_w1(1, b, b != 0) for b in range(R_PASSES)]
+        quantise_w1(1, 0, second[0])
+        for a in range(K_PASSES):
+            nc.vector.tensor_copy(v_codes[:, a, :], tab_raw[a][:].bitcast(U32).indirect(offsets[:]))
+            quantise_w1(1, a + 1, second[a + 1])
+
+        slope = [keep.tile([P, PACK, S], F32, name="slope%d" % b) for b in range(R_PASSES)]
+        slices = [(b, t) for b in range(R_PASSES) for t in range(PACK)]
+
+        def first_product(i):
+            b, t = slices[i]
+            cols = slice(PASS * b + P * t, PASS * b + P * (t + 1))
+            acc = psum.tile([P, S], F32, name="acc", tag="bank%d" % (i % 4))
+            for a in range(K_PASSES):
+                nc.tensor.matmul_mx(
+                    acc[:],
+                    lhsT=w1_codes[:, a, cols].bitcast(FP8X4),
+                    lhsT_scale=w1_plane[:, a, cols],
+                    rhs=v_codes[:, a, :].bitcast(FP8X4),
+                    rhs_scale=v_plane[TAB_PLANE + 4 * a : P, :],
+                    start=(a == 0),
+                    stop=(a == K_PASSES - 1),
+                )
+            nc.scalar.activation(slope[b][:, t, :], acc[:], ACT.Tanh)
+
+        def square(i):
+            b, t = slices[i]
+            nc.scalar.activation(slope[b][:, t, :], slope[b][:, t, :], ACT.Square)
+
+        def affine(i):
+            b, t = slices[i]
+            nc.scalar.activation(
+                slope[b][:, t, :],
+                slope[b][:, t, :],
+                ACT.Identity,
+                bias=gain_sb[:, b, t : t + 1],
+                scale=neg_gain[:, b, t : t + 1],
+            )
+
+        for i in range(len(slices) + 2):
+            if i < len(slices):
+                first_product(i)
+            if 1 <= i <= len(slices):
+                square(i - 1)
+            if i >= 2:
+                affine(i - 2)
+
+        banks = {}
+        for h in range(2):
+            for g in range(K_PASSES):
+                for u in range(2):
+                    banks[h, g, u] = psum.tile(
+                        [P, 2, HALF], F32, name="y_acc", tag="bank%d" % (4 * (1 - h) + 2 * g + u)
+                    )
+        y_plane = keep.tile([P, K_PASSES, S], U8, name="y_plane", align_bytes=64)
+
+        def finish_half(h):
+            cols = slice(HALF * h, HALF * (h + 1))
+            y = big.tile([P, K_PASSES, PACK, HALF], F32, name="y", tag="big")
+            y_codes = keep.tile([P, K_PASSES, HALF], U32, name="y_codes%d" % h, align_bytes=64)
+            grouped = []
+            for g in range(K_PASSES):
+                out_rows = out_0[PASS * g : PASS * (g + 1), cols].rearrange("(p t) m -> p t m", t=PACK)
+                for u in range(2):
+                    nc.scalar.copy(y[:, g, 2 * u : 2 * u + 2, :], banks[h, g, u][:])
+                    nc.sync.dma_start(out_rows[:, 2 * u : 2 * u + 2, :], y[:, g, 2 * u : 2 * u + 2, :])
+                tile = stage.tile([P, HALF * PACK], BF16, name="y_grouped", tag="stage", align_bytes=64)
+                nc.vector.tensor_copy(
+                    tile[:].rearrange("p (c i t) -> p c t i", i=4, t=PACK),
+                    y[:, g, :, :].rearrange("p t (c i) -> p c t i", i=4),
+                )
+                grouped.append(tile)
+            for g in range(K_PASSES):
+                nc.vector.quantize_mx(y_codes[:, g, :].bitcast(FP8X4), y_plane[:, g, cols], grouped[g][:])
+            nc.sync.dma_start(
+                out_1.rearrange("g p m t -> p g (m t)")[:, :, PACK * HALF * h : PACK * HALF * (h + 1)].bitcast(I32),
+                y_codes[:].bitcast(I32),
+            )
+
+        def second_product(b, h, grouped):
+            d_codes = keep.tile([P, HALF], U32, name="d_codes%d_%d" % (b, h), align_bytes=64)
+            d_plane = keep.tile([P, HALF], U8, name="d_plane%d_%d" % (b, h), align_bytes=64)
+            nc.vector.quantize_mx(d_codes[:].bitcast(FP8X4), d_plane[:], grouped[:])
+            for g in range(K_PASSES):
+                for t in range(PACK):
+                    n0 = PASS * g + P * t
+                    nc.tensor.matmul_mx(
+                        banks[h, g, t // 2][:, t % 2, :],
+                        lhsT=wt_codes[:, b, 2 * n0 : 2 * (n0 + P)].bitcast(FP4X4),
+                        lhsT_scale=wt_plane[:, b, n0 : n0 + P],
+                        rhs=d_codes[:].bitcast(FP8X4),
+                        rhs_scale=d_plane[:],
+                        start=(b == 0 and t % 2 == 0),
+                        stop=(b == R_PASSES - 1 and t % 2 == 1),
+                    )
+
+        def load_window(b, t):
+            window = rows.tile([P, T], F32, name="window")
+            g_rows = gT[PASS * b : PASS * (b + 1), :].rearrange("(p t) c -> p t c", t=PACK)
+            nc.sync.dma_start(window[:], g_rows[:, t, :])
+            return window
+
+        def half_list(h):
+            return offsets[:, HALF // 16 * h : HALF // 16 * (h + 1)]
+
+        for b in range(R_PASSES):
+            last = b == R_PASSES - 1
+            slots = PACK - 1 if last else PACK
+            picked = [keep.tile([P, slots, HALF], F32, name="picked%d_%d" % (b, h)) for h in range(2)]
+            for t in range(slots):
+                window = load_window(b, t)
+                for h in range(2):
+                    nc.vector.tensor_copy(picked[h][:, t, :], window[:].indirect(half_list(h)))
+            grouped = []
+            for h in range(2):
+                tile = stage.tile([P, HALF * PACK], BF16, name="delta", tag="stage", align_bytes=64)
+                nc.vector.tensor_tensor(
+                    tile[:].rearrange("p (c i t) -> p c t i", i=4, t=PACK)[:, :, 0:slots, :],
+                    slope[b][:, 0:slots, HALF * h : HALF * (h + 1)].rearrange("p t (c i) -> p c t i", i=4),
+                    picked[h][:].rearrange("p t (c i) -> p c t i", i=4),
+                    ALU.mult,
+                )
+                grouped.append(tile)
+            if last:
+                window = load_window(b, slots)
+            for h in range(2):
+                if last:
+                    product = keep.tile([P, HALF], F32, name="product")
+                    nc.vector.tensor_tensor(
+                        product[:],
+                        window[:].indirect(half_list(h)),
+                        slope[b][:, slots, HALF * h : HALF * (h + 1)],
+                        ALU.mult,
+                    )
+                    nc.vector.tensor_copy(grouped[h][:].rearrange("p (m t) -> p m t", t=PACK)[:, :, slots], product[:])
+                second_product(b, h, grouped[h])
+        for h in range(2):
+            finish_half(h)
+        for q in range(4):
+            nc.sync.dma_start(
+                out_2[:, 4 * q : 4 * q + 4, :].rearrange("g r m -> r g m").bitcast(I32),
+                y_plane[32 * q : 32 * q + 4, :, :].bitcast(I32),
+            )

@@ -1,6 +1,7 @@
 from contextlib import ExitStack
 
 import concourse.mybir as mybir
+from concourse.masks import make_identity
 
 K, H, T, S = 1024, 1536, 2048, 512
 FLOPS = 2 * K * H * S * 2
@@ -41,35 +42,74 @@ def tile_list_recomputed_tanh_backprop_kernel(
         wt_raw = keep.tile([P, R_PASSES, 2 * K], U8, name="wt_raw")
         wt_raw_scales = keep.tile([P, R_PASSES, K], U8, name="wt_raw_scales")
         tab_raw_scales = keep.tile([P, T], U8, name="tab_raw_scales")
-        gain_sb = keep.tile([P, R_PASSES, PACK], F32, name="gain_sb")
-        neg_gain = keep.tile([P, R_PASSES, PACK], F32, name="neg_gain")
+        gain_rows = keep.tile([P, PASS], F32, name="gain_rows")
+        identity = keep.tile([P, P], F32, name="identity")
+        gain_sb = keep.tile([P, PACK, R_PASSES], F32, name="gain_sb")
+        neg_gain = keep.tile([P, PACK, R_PASSES], F32, name="neg_gain")
 
-        nc.vector.memset(wt_raw_scales[:].bitcast(I32), 0)
         nc.vector.memset(tab_raw_scales[:].bitcast(I32), 0)
+        nc.vector.memset(gain_rows[:], 0.0)
+        nc.vector.memset(wt_raw_scales[:].bitcast(I32), 0)
+        make_identity(nc, identity[:])
 
+        def load_w1(a, pool, tag, c0, c1):
+            raw = pool.tile([P, PACK, c1 - c0], F32, name="w1_raw", tag=tag)
+            nc.sync.dma_start(raw[:], w1[PASS * a : PASS * (a + 1), c0:c1].rearrange("(p j) r -> p j r", j=PACK))
+            return raw
+
+        w1_head = [load_w1(a, big, "big", 0, PASS) for a in range(K_PASSES)]
+        nc.sync.dma_start(offsets[:], offs)
+        for q in range(4):
+            nc.sync.dma_start(
+                tab_raw_scales[32 * q + TAB_PLANE : 32 * q + TAB_PLANE + 4 * K_PASSES, :].bitcast(I32),
+                tab_scales[:, 4 * q : 4 * q + 4, :].bitcast(I32),
+            )
+        nc.sync.dma_start(gain_rows[0:R_PASSES, :], gain.rearrange("(b c) -> b c", c=PASS))
+        tab_raw = []
+        for a in range(K_PASSES):
+            raw = keep.tile([P, T], I32, name="tab_raw%d" % a)
+            nc.sync.dma_start(raw[:], tab_words[a].rearrange("p t i -> p (t i)").bitcast(I32))
+            tab_raw.append(raw)
         nc.sync.dma_start(wt_raw[:].bitcast(I32), wt_words.rearrange("a p c -> p a c").bitcast(I32))
         for q in range(4):
             nc.sync.dma_start(
                 wt_raw_scales[32 * q : 32 * q + 4, :, :].bitcast(I32),
                 wt_scales[:, 4 * q : 4 * q + 4, :].rearrange("a r c -> r a c").bitcast(I32),
             )
-        nc.sync.dma_start(offsets[:], offs)
-        w1_raw = []
+        w1_rest = [load_w1(a, keep, "w1_rest%d" % a, PASS, H) for a in range(K_PASSES)]
+
+        turned = psum.tile([P, PACK, P], F32, name="turned", tag="bank7")
+        for t in range(PACK):
+            nc.tensor.transpose(turned[:, t, :], gain_rows[:].rearrange("p (m t) -> p t m", t=PACK)[:, t, :], identity[:])
+        nc.scalar.copy(gain_sb[:], turned[:, :, 0:R_PASSES])
+        nc.scalar.activation(neg_gain[:], turned[:, :, 0:R_PASSES], ACT.Copy, scale=-1.0)
+
+        w1_codes = keep.tile([P, K_PASSES, H], U32, name="w1_codes", align_bytes=64)
+        w1_plane = keep.tile([P, K_PASSES, H], U8, name="w1_plane", align_bytes=64)
+        v_codes = keep.tile([P, K_PASSES, S], U32, name="v_codes", align_bytes=64)
+        v_plane = keep.tile([P, S], U8, name="v_plane", align_bytes=64)
+
+        def round_w1(a, b, on_scalar):
+            raw = w1_head[a][:] if b == 0 else w1_rest[a][:, :, PASS * (b - 1) : PASS * b]
+            grouped = stage.tile([P, PASS * PACK], BF16, name="grouped", tag="stage", align_bytes=64)
+            dst = grouped[:].rearrange("p (t m j) -> p m t j", t=PACK, j=PACK)
+            src = raw.rearrange("p j (m t) -> p m t j", t=PACK)
+            if on_scalar:
+                nc.scalar.copy(dst, src)
+            else:
+                nc.vector.tensor_copy(dst, src)
+            return grouped
+
+        def quantise_w1(a, b, grouped):
+            cols = slice(PASS * b, PASS * (b + 1))
+            nc.vector.quantize_mx(w1_codes[:, a, cols].bitcast(FP8X4), w1_plane[:, a, cols], grouped[:])
+
+        head = [round_w1(a, 0, a == 0) for a in range(K_PASSES)]
+        nc.vector.tensor_copy(v_plane[:], tab_raw_scales[:].indirect(offsets[:]))
         for a in range(K_PASSES):
-            raw = big.tile([P, PACK, H], F32, name="w1_raw", tag="big")
-            nc.sync.dma_start(raw[:], w1[PASS * a : PASS * (a + 1), :].rearrange("(p j) r -> p j r", j=PACK))
-            w1_raw.append(raw)
-        nc.sync.dma_start(gain_sb[:], gain.rearrange("(b p t) -> p b t", p=P, t=PACK))
-        for q in range(4):
-            nc.sync.dma_start(
-                tab_raw_scales[32 * q + TAB_PLANE : 32 * q + TAB_PLANE + 4 * K_PASSES, :].bitcast(I32),
-                tab_scales[:, 4 * q : 4 * q + 4, :].bitcast(I32),
-            )
-        tab_raw = []
+            quantise_w1(a, 0, head[a])
         for a in range(K_PASSES):
-            raw = keep.tile([P, T], I32, name="tab_raw%d" % a)
-            nc.sync.dma_start(raw[:], tab_words[a].rearrange("p t i -> p (t i)").bitcast(I32))
-            tab_raw.append(raw)
+            nc.vector.tensor_copy(v_codes[:, a, :], tab_raw[a][:].bitcast(U32).indirect(offsets[:]))
 
         wt_codes = keep.tile([P, R_PASSES, 2 * K], U8, name="wt_codes", align_bytes=64)
         wt_plane = keep.tile([P, R_PASSES, K], U8, name="wt_plane", align_bytes=64)
@@ -83,44 +123,17 @@ def tile_list_recomputed_tanh_backprop_kernel(
                 wt_plane[:, b, :].rearrange("p (g t q) -> p g t q", t=PACK, q=P),
                 wt_raw_scales[:, b, :].rearrange("p (g q t) -> p g t q", t=PACK, q=P),
             )
-        nc.vector.tensor_scalar(neg_gain[:], gain_sb[:], -1.0, None, ALU.mult)
 
-        w1_codes = keep.tile([P, K_PASSES, H], U32, name="w1_codes", align_bytes=64)
-        w1_plane = keep.tile([P, K_PASSES, H], U8, name="w1_plane", align_bytes=64)
-        v_codes = keep.tile([P, K_PASSES, S], U32, name="v_codes", align_bytes=64)
-        v_plane = keep.tile([P, S], U8, name="v_plane", align_bytes=64)
-
-        def round_w1(a, b, on_scalar):
-            grouped = stage.tile([P, PASS * PACK], BF16, name="grouped", tag="stage", align_bytes=64)
-            dst = grouped[:].rearrange("p (t m j) -> p m t j", t=PACK, j=PACK)
-            src = w1_raw[a][:, :, PASS * b : PASS * (b + 1)].rearrange("p j (m t) -> p m t j", t=PACK)
-            if on_scalar:
-                nc.scalar.copy(dst, src)
-            else:
-                nc.vector.tensor_copy(dst, src)
-            return grouped
-
-        def quantise_w1(a, b, grouped):
-            cols = slice(PASS * b, PASS * (b + 1))
-            nc.vector.quantize_mx(w1_codes[:, a, cols].bitcast(FP8X4), w1_plane[:, a, cols], grouped[:])
-
-        first = [round_w1(0, b, b == 0) for b in range(R_PASSES)]
-        nc.vector.tensor_copy(v_plane[:], tab_raw_scales[:].indirect(offsets[:]))
-        for b in (1, 2, 0):
-            quantise_w1(0, b, first[b])
-        second = [round_w1(1, b, b != 0) for b in range(R_PASSES)]
-        quantise_w1(1, 0, second[0])
         for a in range(K_PASSES):
-            nc.vector.tensor_copy(v_codes[:, a, :], tab_raw[a][:].bitcast(U32).indirect(offsets[:]))
-            quantise_w1(1, a + 1, second[a + 1])
+            rest = [round_w1(a, b, a == 1 and b == 2) for b in range(1, R_PASSES)]
+            for b in range(1, R_PASSES):
+                quantise_w1(a, b, rest[b - 1])
 
         slope = [keep.tile([P, PACK, S], F32, name="slope%d" % b) for b in range(R_PASSES)]
-        slices = [(b, t) for b in range(R_PASSES) for t in range(PACK)]
 
-        def first_product(i):
-            b, t = slices[i]
+        def first_product(b, t):
             cols = slice(PASS * b + P * t, PASS * b + P * (t + 1))
-            acc = psum.tile([P, S], F32, name="acc", tag="bank%d" % (i % 4))
+            acc = psum.tile([P, S], F32, name="acc", tag="bank%d" % t)
             for a in range(K_PASSES):
                 nc.tensor.matmul_mx(
                     acc[:],
@@ -133,64 +146,65 @@ def tile_list_recomputed_tanh_backprop_kernel(
                 )
             nc.scalar.activation(slope[b][:, t, :], acc[:], ACT.Tanh)
 
-        def square(i):
-            b, t = slices[i]
+        def square(b, t):
             nc.scalar.activation(slope[b][:, t, :], slope[b][:, t, :], ACT.Square)
 
-        def affine(i):
-            b, t = slices[i]
+        def affine(b, t):
             nc.scalar.activation(
                 slope[b][:, t, :],
                 slope[b][:, t, :],
                 ACT.Identity,
-                bias=gain_sb[:, b, t : t + 1],
-                scale=neg_gain[:, b, t : t + 1],
+                bias=gain_sb[:, t, b : b + 1],
+                scale=neg_gain[:, t, b : b + 1],
             )
 
-        for i in range(len(slices) + 2):
-            if i < len(slices):
-                first_product(i)
-            if 1 <= i <= len(slices):
-                square(i - 1)
-            if i >= 2:
-                affine(i - 2)
+        def make_slope(b):
+            for i in range(PACK + 2):
+                if i < PACK:
+                    first_product(b, i)
+                if 1 <= i <= PACK:
+                    square(b, i - 1)
+                if i >= 2:
+                    affine(b, i - 2)
 
         banks = {}
-        for h in range(2):
+
+        def open_banks(h):
             for g in range(K_PASSES):
                 for u in range(2):
                     banks[h, g, u] = psum.tile(
                         [P, 2, HALF], F32, name="y_acc", tag="bank%d" % (4 * (1 - h) + 2 * g + u)
                     )
-        y_plane = keep.tile([P, K_PASSES, S], U8, name="y_plane", align_bytes=64)
 
-        def finish_half(h):
-            cols = slice(HALF * h, HALF * (h + 1))
-            y = big.tile([P, K_PASSES, PACK, HALF], F32, name="y", tag="big")
-            y_codes = keep.tile([P, K_PASSES, HALF], U32, name="y_codes%d" % h, align_bytes=64)
-            grouped = []
-            for g in range(K_PASSES):
-                out_rows = out_0[PASS * g : PASS * (g + 1), cols].rearrange("(p t) m -> p t m", t=PACK)
-                for u in range(2):
-                    nc.scalar.copy(y[:, g, 2 * u : 2 * u + 2, :], banks[h, g, u][:])
-                    nc.sync.dma_start(out_rows[:, 2 * u : 2 * u + 2, :], y[:, g, 2 * u : 2 * u + 2, :])
-                tile = stage.tile([P, HALF * PACK], BF16, name="y_grouped", tag="stage", align_bytes=64)
-                nc.vector.tensor_copy(
-                    tile[:].rearrange("p (c i t) -> p c t i", i=4, t=PACK),
-                    y[:, g, :, :].rearrange("p t (c i) -> p c t i", i=4),
-                )
-                grouped.append(tile)
-            for g in range(K_PASSES):
-                nc.vector.quantize_mx(y_codes[:, g, :].bitcast(FP8X4), y_plane[:, g, cols], grouped[g][:])
-            nc.sync.dma_start(
-                out_1.rearrange("g p m t -> p g (m t)")[:, :, PACK * HALF * h : PACK * HALF * (h + 1)].bitcast(I32),
-                y_codes[:].bitcast(I32),
+        def load_window(b, t):
+            window = rows.tile([P, T], F32, name="window")
+            g_rows = gT[PASS * b : PASS * (b + 1), :].rearrange("(p t) c -> p t c", t=PACK)
+            nc.sync.dma_start(window[:], g_rows[:, t, :])
+            return window
+
+        def pick_and_scale(dst, window, b, t, h):
+            nc.vector.tensor_tensor(
+                dst,
+                window[:].indirect(offsets[:, HALF // 16 * h : HALF // 16 * (h + 1)]),
+                slope[b][:, t, HALF * h : HALF * (h + 1)],
+                ALU.mult,
             )
 
-        def second_product(b, h, grouped):
+        def interleave(dst, src, on_scalar):
+            dst = dst.rearrange("p (c i t) -> p c t i", i=4, t=PACK)
+            src = src.rearrange("p t (c i) -> p c t i", i=4)
+            if on_scalar:
+                nc.scalar.copy(dst, src)
+            else:
+                nc.vector.tensor_copy(dst, src)
+
+        def quantise_delta(b, h, grouped):
             d_codes = keep.tile([P, HALF], U32, name="d_codes%d_%d" % (b, h), align_bytes=64)
             d_plane = keep.tile([P, HALF], U8, name="d_plane%d_%d" % (b, h), align_bytes=64)
-            nc.vector.quantize_mx(d_codes[:].bitcast(FP8X4), d_plane[:], grouped[:])
+            nc.vector.quantize_mx(d_codes[:].bitcast(FP8X4), d_plane[:], grouped)
+            return d_codes, d_plane
+
+        def second_product(b, h, d_codes, d_plane):
             for g in range(K_PASSES):
                 for t in range(PACK):
                     n0 = PASS * g + P * t
@@ -204,46 +218,74 @@ def tile_list_recomputed_tanh_backprop_kernel(
                         stop=(b == R_PASSES - 1 and t % 2 == 1),
                     )
 
-        def load_window(b, t):
-            window = rows.tile([P, T], F32, name="window")
-            g_rows = gT[PASS * b : PASS * (b + 1), :].rearrange("(p t) c -> p t c", t=PACK)
-            nc.sync.dma_start(window[:], g_rows[:, t, :])
-            return window
-
-        def half_list(h):
-            return offsets[:, HALF // 16 * h : HALF // 16 * (h + 1)]
-
-        for b in range(R_PASSES):
-            last = b == R_PASSES - 1
-            slots = PACK - 1 if last else PACK
-            picked = [keep.tile([P, slots, HALF], F32, name="picked%d_%d" % (b, h)) for h in range(2)]
-            for t in range(slots):
+        def make_delta(b, on_scalar):
+            delta = [keep.tile([P, PACK, HALF], F32, name="delta", tag="delta%d_%d" % (b, h)) for h in range(2)]
+            for t in range(PACK):
                 window = load_window(b, t)
                 for h in range(2):
-                    nc.vector.tensor_copy(picked[h][:, t, :], window[:].indirect(half_list(h)))
+                    pick_and_scale(delta[h][:, t, :], window, b, t, h)
+            quantised = []
             grouped = []
             for h in range(2):
-                tile = stage.tile([P, HALF * PACK], BF16, name="delta", tag="stage", align_bytes=64)
-                nc.vector.tensor_tensor(
-                    tile[:].rearrange("p (c i t) -> p c t i", i=4, t=PACK)[:, :, 0:slots, :],
-                    slope[b][:, 0:slots, HALF * h : HALF * (h + 1)].rearrange("p t (c i) -> p c t i", i=4),
-                    picked[h][:].rearrange("p t (c i) -> p c t i", i=4),
-                    ALU.mult,
-                )
+                tile = stage.tile([P, HALF * PACK], BF16, name="d_grouped", tag="stage", align_bytes=64)
+                interleave(tile[:], delta[h][:], on_scalar)
                 grouped.append(tile)
-            if last:
-                window = load_window(b, slots)
             for h in range(2):
-                if last:
-                    product = keep.tile([P, HALF], F32, name="product")
-                    nc.vector.tensor_tensor(
-                        product[:],
-                        window[:].indirect(half_list(h)),
-                        slope[b][:, slots, HALF * h : HALF * (h + 1)],
-                        ALU.mult,
-                    )
-                    nc.vector.tensor_copy(grouped[h][:].rearrange("p (m t) -> p m t", t=PACK)[:, :, slots], product[:])
-                second_product(b, h, grouped[h])
+                quantised.append(quantise_delta(b, h, grouped[h][:]))
+            return quantised
+
+        make_slope(0)
+        make_slope(1)
+        open_banks(0)
+        early = [make_delta(0, True)]
+        second_product(0, 0, *early[0][0])
+        make_slope(2)
+        open_banks(1)
+        second_product(0, 1, *early[0][1])
+        early.append(make_delta(1, False))
+        for h in range(2):
+            second_product(1, h, *early[1][h])
+
+        b = R_PASSES - 1
+        delta_a = keep.tile([P, PACK, HALF], F32, name="delta_a")
+        delta_b = keep.tile([P, PACK + 1, HALF], F32, name="delta_b", align_bytes=64)
+        for t in range(PACK - 1):
+            window = load_window(b, t)
+            pick_and_scale(delta_a[:, t, :], window, b, t, 0)
+            pick_and_scale(delta_b[:, t, :], window, b, t, 1)
+        t = PACK - 1
+        window = load_window(b, t)
+        pick_and_scale(delta_a[:, t, :], window, b, t, 0)
+        borrowed = delta_b[:, t : t + 2, :].rearrange("p s c -> p (s c)").bitcast(BF16)
+        interleave(borrowed, delta_a[:], False)
+        second_product(b, 0, *quantise_delta(b, 0, borrowed))
+        pick_and_scale(delta_b[:, t, :], window, b, t, 1)
+        tile = stage.tile([P, HALF * PACK], BF16, name="d_grouped", tag="stage", align_bytes=64)
+        interleave(tile[:], delta_b[:, 0:PACK, :], False)
+        second_product(b, 1, *quantise_delta(b, 1, tile[:]))
+
+        y_plane = keep.tile([P, K_PASSES, S], U8, name="y_plane", align_bytes=64)
+
+        def finish_half(h):
+            cols = slice(HALF * h, HALF * (h + 1))
+            y = big.tile([P, K_PASSES, PACK, HALF], F32, name="y", tag="big")
+            y_codes = keep.tile([P, K_PASSES, HALF], U32, name="y_codes%d" % h, align_bytes=64)
+            grouped = []
+            for g in range(K_PASSES):
+                out_rows = out_0[PASS * g : PASS * (g + 1), cols].rearrange("(p t) m -> p t m", t=PACK)
+                for u in range(2):
+                    nc.scalar.copy(y[:, g, 2 * u : 2 * u + 2, :], banks[h, g, u][:])
+                    nc.sync.dma_start(out_rows[:, 2 * u : 2 * u + 2, :], y[:, g, 2 * u : 2 * u + 2, :])
+                tile = stage.tile([P, HALF * PACK], BF16, name="y_grouped", tag="stage", align_bytes=64)
+                interleave(tile[:], y[:, g, :, :], False)
+                grouped.append(tile)
+            for g in range(K_PASSES):
+                nc.vector.quantize_mx(y_codes[:, g, :].bitcast(FP8X4), y_plane[:, g, cols], grouped[g][:])
+            nc.sync.dma_start(
+                out_1.rearrange("g p m t -> p g (m t)")[:, :, PACK * HALF * h : PACK * HALF * (h + 1)].bitcast(I32),
+                y_codes[:].bitcast(I32),
+            )
+
         for h in range(2):
             finish_half(h)
         for q in range(4):

@@ -24,7 +24,7 @@ K_PASSES = K // PASS
 R_PASSES = H // PASS
 HALF = S // 2
 TAB_PLANE = 8
-G_BUFS = 6
+G_BUFS = 4
 
 
 def tile_list_recomputed_tanh_backprop_kernel(
@@ -39,7 +39,8 @@ def tile_list_recomputed_tanh_backprop_kernel(
         psum = ctx.enter_context(tc.psum_pool(name="psum", bufs=1))
 
         offsets = keep.tile([P, S // 16], U16, name="offsets")
-        wt_raw = keep.tile([P, R_PASSES, 2 * K], U8, name="wt_raw")
+        wt_raw = keep.tile([P, R_PASSES - 1, 2 * K], U8, name="wt_raw")
+        wt_rows = wt_words.rearrange("a p c -> p a c")
         wt_raw_scales = keep.tile([P, R_PASSES, K], U8, name="wt_raw_scales")
         tab_raw_scales = keep.tile([P, T], U8, name="tab_raw_scales")
         gain_rows = keep.tile([P, PASS], F32, name="gain_rows")
@@ -48,35 +49,35 @@ def tile_list_recomputed_tanh_backprop_kernel(
         neg_gain = keep.tile([P, PACK, R_PASSES], F32, name="neg_gain")
 
         nc.vector.memset(tab_raw_scales[:].bitcast(I32), 0)
-        nc.vector.memset(gain_rows[:], 0.0)
+        nc.gpsimd.memset(gain_rows[:], 0.0)
         nc.vector.memset(wt_raw_scales[:].bitcast(I32), 0)
         make_identity(nc, identity[:])
 
-        def load_w1(a, pool, tag, c0, c1):
-            raw = pool.tile([P, PACK, c1 - c0], F32, name="w1_raw", tag=tag)
-            nc.sync.dma_start(raw[:], w1[PASS * a : PASS * (a + 1), c0:c1].rearrange("(p j) r -> p j r", j=PACK))
+        def load_w1(a):
+            raw = big.tile([P, PACK, H], F32, name="w1_raw", tag="big")
+            nc.sync.dma_start(raw[:], w1[PASS * a : PASS * (a + 1), :].rearrange("(p j) r -> p j r", j=PACK))
             return raw
 
-        w1_head = [load_w1(a, big, "big", 0, PASS) for a in range(K_PASSES)]
+        nc.sync.dma_start(wt_raw[:].bitcast(I32), wt_rows[:, 0 : R_PASSES - 1, :].bitcast(I32))
+        w1_raw = [load_w1(0)]
         nc.sync.dma_start(offsets[:], offs)
+        nc.sync.dma_start(gain_rows[0:R_PASSES, :], gain.rearrange("(b c) -> b c", c=PASS))
         for q in range(4):
             nc.sync.dma_start(
                 tab_raw_scales[32 * q + TAB_PLANE : 32 * q + TAB_PLANE + 4 * K_PASSES, :].bitcast(I32),
                 tab_scales[:, 4 * q : 4 * q + 4, :].bitcast(I32),
             )
-        nc.sync.dma_start(gain_rows[0:R_PASSES, :], gain.rearrange("(b c) -> b c", c=PASS))
+        w1_raw.append(load_w1(1))
         tab_raw = []
         for a in range(K_PASSES):
-            raw = keep.tile([P, T], I32, name="tab_raw%d" % a)
+            raw = rows.tile([P, T], I32, name="tab_raw", tag="windows")
             nc.sync.dma_start(raw[:], tab_words[a].rearrange("p t i -> p (t i)").bitcast(I32))
             tab_raw.append(raw)
-        nc.sync.dma_start(wt_raw[:].bitcast(I32), wt_words.rearrange("a p c -> p a c").bitcast(I32))
         for q in range(4):
             nc.sync.dma_start(
                 wt_raw_scales[32 * q : 32 * q + 4, :, :].bitcast(I32),
                 wt_scales[:, 4 * q : 4 * q + 4, :].rearrange("a r c -> r a c").bitcast(I32),
             )
-        w1_rest = [load_w1(a, keep, "w1_rest%d" % a, PASS, H) for a in range(K_PASSES)]
 
         turned = psum.tile([P, PACK, P], F32, name="turned", tag="bank7")
         for t in range(PACK):
@@ -84,13 +85,29 @@ def tile_list_recomputed_tanh_backprop_kernel(
         nc.scalar.copy(gain_sb[:], turned[:, :, 0:R_PASSES])
         nc.scalar.activation(neg_gain[:], turned[:, :, 0:R_PASSES], ACT.Copy, scale=-1.0)
 
+        wt_codes = {}
+
+        def deal_wt(b, g, raw, on_scalar):
+            wt_codes[b, g] = keep.tile([P, 2 * PASS], U8, name="wt_codes%d_%d" % (b, g), align_bytes=64)
+            dst = wt_codes[b, g][:].bitcast(U16).rearrange("p (t q) -> p t q", t=PACK)
+            src = raw.bitcast(U16).rearrange("p (q t) -> p t q", t=PACK)
+            if on_scalar:
+                nc.scalar.copy(dst, src)
+            else:
+                nc.vector.tensor_copy(dst, src)
+
+        wt_plane = keep.tile([P, R_PASSES, K], U8, name="wt_plane", align_bytes=64)
+        for b in range(R_PASSES - 1):
+            for g in range(K_PASSES):
+                deal_wt(b, g, wt_raw[:, b, 2 * PASS * g : 2 * PASS * (g + 1)], False)
+
         w1_codes = keep.tile([P, K_PASSES, H], U32, name="w1_codes", align_bytes=64)
         w1_plane = keep.tile([P, K_PASSES, H], U8, name="w1_plane", align_bytes=64)
         v_codes = keep.tile([P, K_PASSES, S], U32, name="v_codes", align_bytes=64)
         v_plane = keep.tile([P, S], U8, name="v_plane", align_bytes=64)
 
         def round_w1(a, b, on_scalar):
-            raw = w1_head[a][:] if b == 0 else w1_rest[a][:, :, PASS * (b - 1) : PASS * b]
+            raw = w1_raw[a][:, :, PASS * b : PASS * (b + 1)]
             grouped = stage.tile([P, PASS * PACK], BF16, name="grouped", tag="stage", align_bytes=64)
             dst = grouped[:].rearrange("p (t m j) -> p m t j", t=PACK, j=PACK)
             src = raw.rearrange("p j (m t) -> p m t j", t=PACK)
@@ -104,30 +121,21 @@ def tile_list_recomputed_tanh_backprop_kernel(
             cols = slice(PASS * b, PASS * (b + 1))
             nc.vector.quantize_mx(w1_codes[:, a, cols].bitcast(FP8X4), w1_plane[:, a, cols], grouped[:])
 
-        head = [round_w1(a, 0, a == 0) for a in range(K_PASSES)]
+        first = [round_w1(0, b, b == 0) for b in range(R_PASSES)]
+        for b in (1, 2, 0):
+            quantise_w1(0, b, first[b])
         nc.vector.tensor_copy(v_plane[:], tab_raw_scales[:].indirect(offsets[:]))
-        for a in range(K_PASSES):
-            quantise_w1(a, 0, head[a])
+        second = [round_w1(1, b, b != 0) for b in range(R_PASSES)]
+        quantise_w1(1, 0, second[0])
         for a in range(K_PASSES):
             nc.vector.tensor_copy(v_codes[:, a, :], tab_raw[a][:].bitcast(U32).indirect(offsets[:]))
+            quantise_w1(1, a + 1, second[a + 1])
 
-        wt_codes = keep.tile([P, R_PASSES, 2 * K], U8, name="wt_codes", align_bytes=64)
-        wt_plane = keep.tile([P, R_PASSES, K], U8, name="wt_plane", align_bytes=64)
-        for b in range(R_PASSES):
-            nc.vector.tensor_copy(
-                wt_codes[:, b, :].bitcast(U16).rearrange("p (g t q) -> p g t q", t=PACK, q=P),
-                wt_raw[:, b, :].bitcast(U16).rearrange("p (g q t) -> p g t q", t=PACK, q=P),
-            )
         for b in range(R_PASSES):
             nc.vector.tensor_copy(
                 wt_plane[:, b, :].rearrange("p (g t q) -> p g t q", t=PACK, q=P),
                 wt_raw_scales[:, b, :].rearrange("p (g q t) -> p g t q", t=PACK, q=P),
             )
-
-        for a in range(K_PASSES):
-            rest = [round_w1(a, b, a == 1 and b == 2) for b in range(1, R_PASSES)]
-            for b in range(1, R_PASSES):
-                quantise_w1(a, b, rest[b - 1])
 
         slope = [keep.tile([P, PACK, S], F32, name="slope%d" % b) for b in range(R_PASSES)]
 
@@ -176,31 +184,28 @@ def tile_list_recomputed_tanh_backprop_kernel(
                         [P, 2, HALF], F32, name="y_acc", tag="bank%d" % (4 * (1 - h) + 2 * g + u)
                     )
 
-        def load_window(b, t):
-            window = rows.tile([P, T], F32, name="window")
+        def load_windows(b, t0, t1):
+            windows = rows.tile([P, t1 - t0, T], F32, name="windows", tag="windows")
             g_rows = gT[PASS * b : PASS * (b + 1), :].rearrange("(p t) c -> p t c", t=PACK)
-            nc.sync.dma_start(window[:], g_rows[:, t, :])
-            return window
+            nc.sync.dma_start(windows[:], g_rows[:, t0:t1, :])
+            return windows
 
-        def pick_and_scale(dst, window, b, t, h):
-            nc.vector.tensor_tensor(
-                dst,
-                window[:].indirect(offsets[:, HALF // 16 * h : HALF // 16 * (h + 1)]),
-                slope[b][:, t, HALF * h : HALF * (h + 1)],
-                ALU.mult,
+        def pick(dst, window, c0, c1):
+            nc.vector.tensor_copy(dst, window.indirect(offsets[:, c0 // 16 : c1 // 16]))
+
+        def interleave(dst, src):
+            nc.vector.tensor_copy(
+                dst.rearrange("p (c i t) -> p c t i", i=4, t=PACK), src.rearrange("p t (c i) -> p c t i", i=4)
             )
 
-        def interleave(dst, src, on_scalar):
-            dst = dst.rearrange("p (c i t) -> p c t i", i=4, t=PACK)
-            src = src.rearrange("p t (c i) -> p c t i", i=4)
-            if on_scalar:
-                nc.scalar.copy(dst, src)
-            else:
-                nc.vector.tensor_copy(dst, src)
+        def pick_and_scale(dst, window, b, t, c0, c1):
+            nc.vector.tensor_tensor(
+                dst, window[:].indirect(offsets[:, c0 // 16 : c1 // 16]), slope[b][:, t, c0:c1], ALU.mult
+            )
 
-        def quantise_delta(b, h, grouped):
-            d_codes = keep.tile([P, HALF], U32, name="d_codes%d_%d" % (b, h), align_bytes=64)
-            d_plane = keep.tile([P, HALF], U8, name="d_plane%d_%d" % (b, h), align_bytes=64)
+        def quantise_delta(name, grouped, width):
+            d_codes = keep.tile([P, width], U32, name=name + "_codes", align_bytes=64)
+            d_plane = keep.tile([P, width], U8, name=name + "_plane", align_bytes=64)
             nc.vector.quantize_mx(d_codes[:].bitcast(FP8X4), d_plane[:], grouped)
             return d_codes, d_plane
 
@@ -210,66 +215,68 @@ def tile_list_recomputed_tanh_backprop_kernel(
                     n0 = PASS * g + P * t
                     nc.tensor.matmul_mx(
                         banks[h, g, t // 2][:, t % 2, :],
-                        lhsT=wt_codes[:, b, 2 * n0 : 2 * (n0 + P)].bitcast(FP4X4),
+                        lhsT=wt_codes[b, g][:, 2 * P * t : 2 * P * (t + 1)].bitcast(FP4X4),
                         lhsT_scale=wt_plane[:, b, n0 : n0 + P],
-                        rhs=d_codes[:].bitcast(FP8X4),
-                        rhs_scale=d_plane[:],
+                        rhs=d_codes.bitcast(FP8X4),
+                        rhs_scale=d_plane,
                         start=(b == 0 and t % 2 == 0),
                         stop=(b == R_PASSES - 1 and t % 2 == 1),
                     )
 
-        def make_delta(b, on_scalar):
-            delta = [keep.tile([P, PACK, HALF], F32, name="delta", tag="delta%d_%d" % (b, h)) for h in range(2)]
-            for t in range(PACK):
-                window = load_window(b, t)
-                for h in range(2):
-                    pick_and_scale(delta[h][:, t, :], window, b, t, h)
-            quantised = []
-            grouped = []
-            for h in range(2):
-                tile = stage.tile([P, HALF * PACK], BF16, name="d_grouped", tag="stage", align_bytes=64)
-                interleave(tile[:], delta[h][:], on_scalar)
-                grouped.append(tile)
-            for h in range(2):
-                quantised.append(quantise_delta(b, h, grouped[h][:]))
-            return quantised
-
-        make_slope(0)
-        make_slope(1)
-        open_banks(0)
-        early = [make_delta(0, True)]
-        second_product(0, 0, *early[0][0])
-        make_slope(2)
-        open_banks(1)
-        second_product(0, 1, *early[0][1])
-        early.append(make_delta(1, False))
+        for b in range(R_PASSES):
+            make_slope(b)
         for h in range(2):
-            second_product(1, h, *early[1][h])
+            open_banks(h)
+        for b in range(R_PASSES - 1):
+            picked = keep.tile([P, PACK, S], F32, name="picked%d" % b)
+            for t0, t1 in ((0, 2), (2, 4)) if b == 0 else ((0, 2), (2, 3), (3, 4)):
+                windows = load_windows(b, t0, t1)
+                for t in range(t0, t1):
+                    pick(picked[:, t, :], windows[:, t - t0, :], 0, S)
+            grouped = stage.tile([P, S * PACK], BF16, name="d_grouped", tag="stage", align_bytes=64)
+            nc.vector.tensor_tensor(
+                grouped[:].rearrange("p (c i t) -> p c t i", i=2, t=PACK),
+                slope[b][:].rearrange("p t (c i) -> p c t i", i=2),
+                picked[:].rearrange("p t (c i) -> p c t i", i=2),
+                ALU.mult,
+            )
+            d_codes, d_plane = quantise_delta("d%d" % b, grouped[:], S)
+            for h in range(2):
+                cols = slice(HALF * h, HALF * (h + 1))
+                second_product(b, h, d_codes[:, cols], d_plane[:, cols])
 
         b = R_PASSES - 1
+        g_rows = gT[PASS * b : PASS * (b + 1), :].rearrange("(p t) c -> p t c", t=PACK)
         delta_a = keep.tile([P, PACK, HALF], F32, name="delta_a")
         delta_b = keep.tile([P, PACK + 1, HALF], F32, name="delta_b", align_bytes=64)
-        for t in range(PACK - 1):
-            window = load_window(b, t)
-            pick_and_scale(delta_a[:, t, :], window, b, t, 0)
-            pick_and_scale(delta_b[:, t, :], window, b, t, 1)
+        for t in range(PACK):
+            window = rows.tile([P, T], F32, name="window", tag="windows")
+            nc.sync.dma_start(window[:], g_rows[:, t, :])
+            pick_and_scale(delta_a[:, t, :], window, b, t, 0, HALF)
+            if t < PACK - 1:
+                pick_and_scale(delta_b[:, t, :], window, b, t, HALF, S)
+        wt_late = rows.tile([P, 2 * K], U8, name="wt_late", tag="windows")
+        nc.sync.dma_start(wt_late[:].bitcast(I32), wt_rows[:, b, :].bitcast(I32))
+        for g in range(K_PASSES):
+            deal_wt(b, g, wt_late[:, 2 * PASS * g : 2 * PASS * (g + 1)], True)
         t = PACK - 1
-        window = load_window(b, t)
-        pick_and_scale(delta_a[:, t, :], window, b, t, 0)
         borrowed = delta_b[:, t : t + 2, :].rearrange("p s c -> p (s c)").bitcast(BF16)
-        interleave(borrowed, delta_a[:], False)
-        second_product(b, 0, *quantise_delta(b, 0, borrowed))
-        pick_and_scale(delta_b[:, t, :], window, b, t, 1)
-        tile = stage.tile([P, HALF * PACK], BF16, name="d_grouped", tag="stage", align_bytes=64)
-        interleave(tile[:], delta_b[:, 0:PACK, :], False)
-        second_product(b, 1, *quantise_delta(b, 1, tile[:]))
+        interleave(borrowed, delta_a[:])
+        d_codes, d_plane = quantise_delta("last_a", borrowed, HALF)
+        second_product(b, 0, d_codes[:], d_plane[:])
+        pick_and_scale(delta_b[:, t, :], window, b, t, HALF, S)
+        grouped = stage.tile([P, HALF * PACK], BF16, name="d_grouped", tag="stage", align_bytes=64)
+        interleave(grouped[:], delta_b[:, 0:PACK, :])
+        d_codes, d_plane = quantise_delta("last_b", grouped[:], HALF)
+        second_product(b, 1, d_codes[:], d_plane[:])
 
         y_plane = keep.tile([P, K_PASSES, S], U8, name="y_plane", align_bytes=64)
+
+        y_codes = [keep.tile([P, S], U32, name="y_codes%d" % g, align_bytes=64) for g in range(K_PASSES)]
 
         def finish_half(h):
             cols = slice(HALF * h, HALF * (h + 1))
             y = big.tile([P, K_PASSES, PACK, HALF], F32, name="y", tag="big")
-            y_codes = keep.tile([P, K_PASSES, HALF], U32, name="y_codes%d" % h, align_bytes=64)
             grouped = []
             for g in range(K_PASSES):
                 out_rows = out_0[PASS * g : PASS * (g + 1), cols].rearrange("(p t) m -> p t m", t=PACK)
@@ -277,14 +284,12 @@ def tile_list_recomputed_tanh_backprop_kernel(
                     nc.scalar.copy(y[:, g, 2 * u : 2 * u + 2, :], banks[h, g, u][:])
                     nc.sync.dma_start(out_rows[:, 2 * u : 2 * u + 2, :], y[:, g, 2 * u : 2 * u + 2, :])
                 tile = stage.tile([P, HALF * PACK], BF16, name="y_grouped", tag="stage", align_bytes=64)
-                interleave(tile[:], y[:, g, :, :], False)
+                interleave(tile[:], y[:, g, :, :])
                 grouped.append(tile)
             for g in range(K_PASSES):
-                nc.vector.quantize_mx(y_codes[:, g, :].bitcast(FP8X4), y_plane[:, g, cols], grouped[g][:])
-            nc.sync.dma_start(
-                out_1.rearrange("g p m t -> p g (m t)")[:, :, PACK * HALF * h : PACK * HALF * (h + 1)].bitcast(I32),
-                y_codes[:].bitcast(I32),
-            )
+                nc.vector.quantize_mx(y_codes[g][:, cols].bitcast(FP8X4), y_plane[:, g, cols], grouped[g][:])
+                if h == 1:
+                    nc.sync.dma_start(out_1[g].rearrange("p m t -> p (m t)").bitcast(I32), y_codes[g][:].bitcast(I32))
 
         for h in range(2):
             finish_half(h)

@@ -22,9 +22,15 @@ PACK = 4
 PASS = P * PACK
 K_PASSES = K // PASS
 R_PASSES = H // PASS
+LAST = R_PASSES - 1
+QUADRANTS = 4
 HALF = S // 2
-TAB_PLANE = 8
-G_BUFS = 4
+QUARTER = S // 4
+TAB_ROW = 8
+WINDOW_BUFS = 4
+STAGE_BUFS = 4
+COPY_RUN = 4
+PRODUCT_RUN = 2
 
 
 def tile_list_recomputed_tanh_backprop_kernel(
@@ -34,12 +40,12 @@ def tile_list_recomputed_tanh_backprop_kernel(
     with ExitStack() as ctx:
         keep = ctx.enter_context(tc.tile_pool(name="keep", bufs=1))
         big = ctx.enter_context(tc.tile_pool(name="big", bufs=2))
-        stage = ctx.enter_context(tc.tile_pool(name="stage", bufs=4))
-        rows = ctx.enter_context(tc.tile_pool(name="rows", bufs=G_BUFS))
+        stage = ctx.enter_context(tc.tile_pool(name="stage", bufs=STAGE_BUFS))
+        rows = ctx.enter_context(tc.tile_pool(name="rows", bufs=WINDOW_BUFS))
         psum = ctx.enter_context(tc.psum_pool(name="psum", bufs=1))
 
         offsets = keep.tile([P, S // 16], U16, name="offsets")
-        wt_raw = keep.tile([P, R_PASSES - 1, 2 * K], U8, name="wt_raw")
+        wt_raw = keep.tile([P, LAST, 2 * K], U8, name="wt_raw")
         wt_rows = wt_words.rearrange("a p c -> p a c")
         wt_raw_scales = keep.tile([P, R_PASSES, K], U8, name="wt_raw_scales")
         tab_raw_scales = keep.tile([P, T], U8, name="tab_raw_scales")
@@ -58,13 +64,13 @@ def tile_list_recomputed_tanh_backprop_kernel(
             nc.sync.dma_start(raw[:], w1[PASS * a : PASS * (a + 1), :].rearrange("(p j) r -> p j r", j=PACK))
             return raw
 
-        nc.sync.dma_start(wt_raw[:].bitcast(I32), wt_rows[:, 0 : R_PASSES - 1, :].bitcast(I32))
+        nc.sync.dma_start(wt_raw[:].bitcast(I32), wt_rows[:, 0:LAST, :].bitcast(I32))
         w1_raw = [load_w1(0)]
         nc.sync.dma_start(offsets[:], offs)
         nc.sync.dma_start(gain_rows[0:R_PASSES, :], gain.rearrange("(b c) -> b c", c=PASS))
-        for q in range(4):
+        for q in range(QUADRANTS):
             nc.sync.dma_start(
-                tab_raw_scales[32 * q + TAB_PLANE : 32 * q + TAB_PLANE + 4 * K_PASSES, :].bitcast(I32),
+                tab_raw_scales[32 * q + TAB_ROW : 32 * q + TAB_ROW + 4 * K_PASSES, :].bitcast(I32),
                 tab_scales[:, 4 * q : 4 * q + 4, :].bitcast(I32),
             )
         w1_raw.append(load_w1(1))
@@ -73,7 +79,7 @@ def tile_list_recomputed_tanh_backprop_kernel(
             raw = rows.tile([P, T], I32, name="tab_raw", tag="windows")
             nc.sync.dma_start(raw[:], tab_words[a].rearrange("p t i -> p (t i)").bitcast(I32))
             tab_raw.append(raw)
-        for q in range(4):
+        for q in range(QUADRANTS):
             nc.sync.dma_start(
                 wt_raw_scales[32 * q : 32 * q + 4, :, :].bitcast(I32),
                 wt_scales[:, 4 * q : 4 * q + 4, :].rearrange("a r c -> r a c").bitcast(I32),
@@ -87,45 +93,40 @@ def tile_list_recomputed_tanh_backprop_kernel(
 
         wt_codes = {}
 
-        def deal_wt(b, g, raw, on_scalar):
+        def deal_wt(b, g, raw, copy):
             wt_codes[b, g] = keep.tile([P, 2 * PASS], U8, name="wt_codes%d_%d" % (b, g), align_bytes=64)
-            dst = wt_codes[b, g][:].bitcast(U16).rearrange("p (t q) -> p t q", t=PACK)
-            src = raw.bitcast(U16).rearrange("p (q t) -> p t q", t=PACK)
-            if on_scalar:
-                nc.scalar.copy(dst, src)
-            else:
-                nc.vector.tensor_copy(dst, src)
+            copy(
+                wt_codes[b, g][:].bitcast(U16).rearrange("p (t q) -> p t q", t=PACK),
+                raw[:, 2 * PASS * g : 2 * PASS * (g + 1)].bitcast(U16).rearrange("p (q t) -> p t q", t=PACK),
+            )
 
         wt_plane = keep.tile([P, R_PASSES, K], U8, name="wt_plane", align_bytes=64)
-        for b in range(R_PASSES - 1):
+        for b in range(LAST):
             for g in range(K_PASSES):
-                deal_wt(b, g, wt_raw[:, b, 2 * PASS * g : 2 * PASS * (g + 1)], False)
+                deal_wt(b, g, wt_raw[:, b, :], nc.vector.tensor_copy)
 
         w1_codes = keep.tile([P, K_PASSES, H], U32, name="w1_codes", align_bytes=64)
         w1_plane = keep.tile([P, K_PASSES, H], U8, name="w1_plane", align_bytes=64)
         v_codes = keep.tile([P, K_PASSES, S], U32, name="v_codes", align_bytes=64)
         v_plane = keep.tile([P, S], U8, name="v_plane", align_bytes=64)
 
-        def round_w1(a, b, on_scalar):
-            raw = w1_raw[a][:, :, PASS * b : PASS * (b + 1)]
+        def round_w1(a, b, copy):
             grouped = stage.tile([P, PASS * PACK], BF16, name="grouped", tag="stage", align_bytes=64)
-            dst = grouped[:].rearrange("p (t m j) -> p m t j", t=PACK, j=PACK)
-            src = raw.rearrange("p j (m t) -> p m t j", t=PACK)
-            if on_scalar:
-                nc.scalar.copy(dst, src)
-            else:
-                nc.vector.tensor_copy(dst, src)
+            copy(
+                grouped[:].rearrange("p (t m j) -> p m t j", t=PACK, j=PACK),
+                w1_raw[a][:, :, PASS * b : PASS * (b + 1)].rearrange("p j (m t) -> p m t j", t=PACK),
+            )
             return grouped
 
         def quantise_w1(a, b, grouped):
             cols = slice(PASS * b, PASS * (b + 1))
             nc.vector.quantize_mx(w1_codes[:, a, cols].bitcast(FP8X4), w1_plane[:, a, cols], grouped[:])
 
-        first = [round_w1(0, b, b == 0) for b in range(R_PASSES)]
+        first = [round_w1(0, b, nc.scalar.copy if b == 0 else nc.vector.tensor_copy) for b in range(R_PASSES)]
         for b in (1, 2, 0):
             quantise_w1(0, b, first[b])
         nc.vector.tensor_copy(v_plane[:], tab_raw_scales[:].indirect(offsets[:]))
-        second = [round_w1(1, b, b != 0) for b in range(R_PASSES)]
+        second = [round_w1(1, b, nc.vector.tensor_copy if b == 0 else nc.scalar.copy) for b in range(R_PASSES)]
         quantise_w1(1, 0, second[0])
         for a in range(K_PASSES):
             nc.vector.tensor_copy(v_codes[:, a, :], tab_raw[a][:].bitcast(U32).indirect(offsets[:]))
@@ -148,7 +149,7 @@ def tile_list_recomputed_tanh_backprop_kernel(
                     lhsT=w1_codes[:, a, cols].bitcast(FP8X4),
                     lhsT_scale=w1_plane[:, a, cols],
                     rhs=v_codes[:, a, :].bitcast(FP8X4),
-                    rhs_scale=v_plane[TAB_PLANE + 4 * a : P, :],
+                    rhs_scale=v_plane[TAB_ROW + 4 * a : P, :],
                     start=(a == 0),
                     stop=(a == K_PASSES - 1),
                 )
@@ -157,7 +158,7 @@ def tile_list_recomputed_tanh_backprop_kernel(
         def square(b, t):
             nc.scalar.activation(slope[b][:, t, :], slope[b][:, t, :], ACT.Square)
 
-        def affine(b, t):
+        def gain_times_one_minus(b, t):
             nc.scalar.activation(
                 slope[b][:, t, :],
                 slope[b][:, t, :],
@@ -166,48 +167,39 @@ def tile_list_recomputed_tanh_backprop_kernel(
                 scale=neg_gain[:, t, b : b + 1],
             )
 
-        def make_slope(b):
+        for b in range(R_PASSES):
             for i in range(PACK + 2):
                 if i < PACK:
                     first_product(b, i)
                 if 1 <= i <= PACK:
                     square(b, i - 1)
                 if i >= 2:
-                    affine(b, i - 2)
+                    gain_times_one_minus(b, i - 2)
 
         banks = {}
-
-        def open_banks(h):
+        for h in range(2):
             for g in range(K_PASSES):
                 for u in range(2):
                     banks[h, g, u] = psum.tile(
                         [P, 2, HALF], F32, name="y_acc", tag="bank%d" % (4 * (1 - h) + 2 * g + u)
                     )
 
-        def load_windows(b, t0, t1):
-            windows = rows.tile([P, t1 - t0, T], F32, name="windows", tag="windows")
-            g_rows = gT[PASS * b : PASS * (b + 1), :].rearrange("(p t) c -> p t c", t=PACK)
-            nc.sync.dma_start(windows[:], g_rows[:, t0:t1, :])
-            return windows
+        def g_rows(b):
+            return gT[PASS * b : PASS * (b + 1), :].rearrange("(p t) c -> p t c", t=PACK)
 
-        def pick(dst, window, c0, c1):
-            nc.vector.tensor_copy(dst, window.indirect(offsets[:, c0 // 16 : c1 // 16]))
+        def slice_major(ap, run):
+            return ap.rearrange("p t (c i) -> p c t i", i=run)
 
-        def interleave(dst, src):
-            nc.vector.tensor_copy(
-                dst.rearrange("p (c i t) -> p c t i", i=4, t=PACK), src.rearrange("p t (c i) -> p c t i", i=4)
-            )
+        def word_major(ap, run):
+            return ap.rearrange("p (c i t) -> p c t i", i=run, t=PACK)
 
-        def pick_and_scale(dst, window, b, t, c0, c1):
+        def interleave(dst, src, copy):
+            copy(word_major(dst, COPY_RUN), slice_major(src, COPY_RUN))
+
+        def pick_and_scale(dst, window, t, c0, c1):
             nc.vector.tensor_tensor(
-                dst, window[:].indirect(offsets[:, c0 // 16 : c1 // 16]), slope[b][:, t, c0:c1], ALU.mult
+                dst, window[:].indirect(offsets[:, c0 // 16 : c1 // 16]), slope[LAST][:, t, c0:c1], ALU.mult
             )
-
-        def quantise_delta(name, grouped, width):
-            d_codes = keep.tile([P, width], U32, name=name + "_codes", align_bytes=64)
-            d_plane = keep.tile([P, width], U8, name=name + "_plane", align_bytes=64)
-            nc.vector.quantize_mx(d_codes[:].bitcast(FP8X4), d_plane[:], grouped)
-            return d_codes, d_plane
 
         def second_product(b, h, d_codes, d_plane):
             for g in range(K_PASSES):
@@ -220,80 +212,85 @@ def tile_list_recomputed_tanh_backprop_kernel(
                         rhs=d_codes.bitcast(FP8X4),
                         rhs_scale=d_plane,
                         start=(b == 0 and t % 2 == 0),
-                        stop=(b == R_PASSES - 1 and t % 2 == 1),
+                        stop=(b == LAST and t % 2 == 1),
                     )
 
-        for b in range(R_PASSES):
-            make_slope(b)
-        for h in range(2):
-            open_banks(h)
-        for b in range(R_PASSES - 1):
+        for b in range(LAST):
             picked = keep.tile([P, PACK, S], F32, name="picked%d" % b)
-            for t0, t1 in ((0, 2), (2, 4)) if b == 0 else ((0, 2), (2, 3), (3, 4)):
-                windows = load_windows(b, t0, t1)
+            for t0, t1 in ((0, 2), (2, 3), (3, 4)) if b == LAST - 1 else ((0, 2), (2, 4)):
+                windows = rows.tile([P, t1 - t0, T], F32, name="windows", tag="windows")
+                nc.sync.dma_start(windows[:], g_rows(b)[:, t0:t1, :])
                 for t in range(t0, t1):
-                    pick(picked[:, t, :], windows[:, t - t0, :], 0, S)
+                    nc.vector.tensor_copy(picked[:, t, :], windows[:, t - t0, :].indirect(offsets[:]))
             grouped = stage.tile([P, S * PACK], BF16, name="d_grouped", tag="stage", align_bytes=64)
             nc.vector.tensor_tensor(
-                grouped[:].rearrange("p (c i t) -> p c t i", i=2, t=PACK),
-                slope[b][:].rearrange("p t (c i) -> p c t i", i=2),
-                picked[:].rearrange("p t (c i) -> p c t i", i=2),
+                word_major(grouped[:], PRODUCT_RUN),
+                slice_major(slope[b][:], PRODUCT_RUN),
+                slice_major(picked[:], PRODUCT_RUN),
                 ALU.mult,
             )
-            d_codes, d_plane = quantise_delta("d%d" % b, grouped[:], S)
+            d_codes = keep.tile([P, S], U32, name="d_codes%d" % b, align_bytes=64)
+            d_plane = keep.tile([P, S], U8, name="d_plane%d" % b, align_bytes=64)
+            nc.vector.quantize_mx(d_codes[:].bitcast(FP8X4), d_plane[:], grouped[:])
             for h in range(2):
                 cols = slice(HALF * h, HALF * (h + 1))
                 second_product(b, h, d_codes[:, cols], d_plane[:, cols])
 
-        b = R_PASSES - 1
-        g_rows = gT[PASS * b : PASS * (b + 1), :].rearrange("(p t) c -> p t c", t=PACK)
+        final = PACK - 1
         delta_a = keep.tile([P, PACK, HALF], F32, name="delta_a")
         delta_b = keep.tile([P, PACK + 1, HALF], F32, name="delta_b", align_bytes=64)
         for t in range(PACK):
             window = rows.tile([P, T], F32, name="window", tag="windows")
-            nc.sync.dma_start(window[:], g_rows[:, t, :])
-            pick_and_scale(delta_a[:, t, :], window, b, t, 0, HALF)
-            if t < PACK - 1:
-                pick_and_scale(delta_b[:, t, :], window, b, t, HALF, S)
+            nc.sync.dma_start(window[:], g_rows(LAST)[:, t, :])
+            if t < final:
+                pick_and_scale(delta_a[:, t, :], window, t, 0, HALF)
+                pick_and_scale(delta_b[:, t, :], window, t, HALF, S)
         wt_late = rows.tile([P, 2 * K], U8, name="wt_late", tag="windows")
-        nc.sync.dma_start(wt_late[:].bitcast(I32), wt_rows[:, b, :].bitcast(I32))
+        nc.sync.dma_start(wt_late[:].bitcast(I32), wt_rows[:, LAST, :].bitcast(I32))
         for g in range(K_PASSES):
-            deal_wt(b, g, wt_late[:, 2 * PASS * g : 2 * PASS * (g + 1)], True)
-        t = PACK - 1
-        borrowed = delta_b[:, t : t + 2, :].rearrange("p s c -> p (s c)").bitcast(BF16)
-        interleave(borrowed, delta_a[:])
-        d_codes, d_plane = quantise_delta("last_a", borrowed, HALF)
-        second_product(b, 0, d_codes[:], d_plane[:])
-        pick_and_scale(delta_b[:, t, :], window, b, t, HALF, S)
-        grouped = stage.tile([P, HALF * PACK], BF16, name="d_grouped", tag="stage", align_bytes=64)
-        interleave(grouped[:], delta_b[:, 0:PACK, :])
-        d_codes, d_plane = quantise_delta("last_b", grouped[:], HALF)
-        second_product(b, 1, d_codes[:], d_plane[:])
+            deal_wt(LAST, g, wt_late, nc.scalar.copy)
+
+        def last_half(h, delta, grouped):
+            d_codes = keep.tile([P, HALF], U32, name="last_codes%d" % h, align_bytes=64)
+            d_plane = keep.tile([P, HALF], U8, name="last_plane%d" % h, align_bytes=64)
+            quarters = [slice(QUARTER * i, QUARTER * (i + 1)) for i in range(2)]
+            for cols in quarters:
+                pick_and_scale(delta[:, final, cols], window, final, HALF * h + cols.start, HALF * h + cols.stop)
+            for i, cols in enumerate(quarters):
+                interleave(grouped[i], delta[:, 0:PACK, cols], nc.vector.tensor_copy)
+            for i, cols in enumerate(quarters):
+                nc.vector.quantize_mx(d_codes[:, cols].bitcast(FP8X4), d_plane[:, cols], grouped[i])
+            second_product(LAST, h, d_codes[:], d_plane[:])
+
+        last_half(0, delta_a, [delta_b[:, final + 1, :].bitcast(BF16), delta_b[:, final, :].bitcast(BF16)])
+        grouped = stage.tile([P, 2, QUARTER * PACK], BF16, name="d_grouped", tag="stage", align_bytes=64)
+        last_half(1, delta_b, [grouped[:, 0, :], grouped[:, 1, :]])
 
         y_plane = keep.tile([P, K_PASSES, S], U8, name="y_plane", align_bytes=64)
-
         y_codes = [keep.tile([P, S], U32, name="y_codes%d" % g, align_bytes=64) for g in range(K_PASSES)]
-
-        def finish_half(h):
+        for h in range(2):
             cols = slice(HALF * h, HALF * (h + 1))
             y = big.tile([P, K_PASSES, PACK, HALF], F32, name="y", tag="big")
-            grouped = []
+            y_grouped = []
             for g in range(K_PASSES):
+                shared = h == 1 and g == K_PASSES - 1
                 out_rows = out_0[PASS * g : PASS * (g + 1), cols].rearrange("(p t) m -> p t m", t=PACK)
                 for u in range(2):
-                    nc.scalar.copy(y[:, g, 2 * u : 2 * u + 2, :], banks[h, g, u][:])
+                    copy = nc.vector.tensor_copy if shared and u == 1 else nc.scalar.copy
+                    copy(y[:, g, 2 * u : 2 * u + 2, :], banks[h, g, u][:])
                     nc.sync.dma_start(out_rows[:, 2 * u : 2 * u + 2, :], y[:, g, 2 * u : 2 * u + 2, :])
                 tile = stage.tile([P, HALF * PACK], BF16, name="y_grouped", tag="stage", align_bytes=64)
-                interleave(tile[:], y[:, g, :, :])
-                grouped.append(tile)
+                if shared:
+                    interleave(tile[:, : QUARTER * PACK], y[:, g, :, :QUARTER], nc.scalar.copy)
+                    interleave(tile[:, QUARTER * PACK :], y[:, g, :, QUARTER:], nc.vector.tensor_copy)
+                else:
+                    interleave(tile[:], y[:, g, :, :], nc.vector.tensor_copy)
+                y_grouped.append(tile)
             for g in range(K_PASSES):
-                nc.vector.quantize_mx(y_codes[g][:, cols].bitcast(FP8X4), y_plane[:, g, cols], grouped[g][:])
+                nc.vector.quantize_mx(y_codes[g][:, cols].bitcast(FP8X4), y_plane[:, g, cols], y_grouped[g][:])
                 if h == 1:
                     nc.sync.dma_start(out_1[g].rearrange("p m t -> p (m t)").bitcast(I32), y_codes[g][:].bitcast(I32))
-
-        for h in range(2):
-            finish_half(h)
-        for q in range(4):
+        for q in range(QUADRANTS):
             nc.sync.dma_start(
                 out_2[:, 4 * q : 4 * q + 4, :].rearrange("g r m -> r g m").bitcast(I32),
                 y_plane[32 * q : 32 * q + 4, :, :].bitcast(I32),

from contextlib import ExitStack

import concourse.mybir as mybir
from concourse.masks import make_identity

K, H, T, S = 1024, 1536, 2048, 512
FLOPS = 2 * K * H * S * 2

F32 = mybir.dt.float32
BF16 = mybir.dt.bfloat16
I32 = mybir.dt.int32
U32 = mybir.dt.uint32
U16 = mybir.dt.uint16
U8 = mybir.dt.uint8
FP8X4 = mybir.dt.float8_e4m3fn_x4
FP4X4 = mybir.dt.float4_e2m1fn_x4
ACT = mybir.ActivationFunctionType
ALU = mybir.AluOpType

P = 128
PACK = 4
PASS = P * PACK
K_PASSES = K // PASS
R_PASSES = H // PASS
LAST = R_PASSES - 1
QUADRANTS = 4
HALF = S // 2
QUARTER = S // 4
TAB_ROW = 8
WINDOW_BUFS = 4
STAGE_BUFS = 4
COPY_RUN = 4
PRODUCT_RUN = 2


def tile_list_recomputed_tanh_backprop_kernel(
    tc, tab_words, tab_scales, offs, w1, gT, gain, wt_words, wt_scales, out_0, out_1, out_2
):
    nc = tc.nc
    with ExitStack() as ctx:
        keep = ctx.enter_context(tc.tile_pool(name="keep", bufs=1))
        big = ctx.enter_context(tc.tile_pool(name="big", bufs=2))
        stage = ctx.enter_context(tc.tile_pool(name="stage", bufs=STAGE_BUFS))
        rows = ctx.enter_context(tc.tile_pool(name="rows", bufs=WINDOW_BUFS))
        psum = ctx.enter_context(tc.psum_pool(name="psum", bufs=1))

        offsets = keep.tile([P, S // 16], U16, name="offsets")
        wt_raw = keep.tile([P, LAST, 2 * K], U8, name="wt_raw")
        wt_rows = wt_words.rearrange("a p c -> p a c")
        wt_raw_scales = keep.tile([P, R_PASSES, K], U8, name="wt_raw_scales")
        tab_raw_scales = keep.tile([P, T], U8, name="tab_raw_scales")
        gain_rows = keep.tile([P, PASS], F32, name="gain_rows")
        identity = keep.tile([P, P], F32, name="identity")
        gain_sb = keep.tile([P, PACK, R_PASSES], F32, name="gain_sb")
        neg_gain = keep.tile([P, PACK, R_PASSES], F32, name="neg_gain")

        nc.vector.memset(tab_raw_scales[:].bitcast(I32), 0)
        nc.gpsimd.memset(gain_rows[:], 0.0)
        nc.vector.memset(wt_raw_scales[:].bitcast(I32), 0)
        make_identity(nc, identity[:])

        def load_w1(a):
            raw = big.tile([P, PACK, H], F32, name="w1_raw", tag="big")
            nc.sync.dma_start(raw[:], w1[PASS * a : PASS * (a + 1), :].rearrange("(p j) r -> p j r", j=PACK))
            return raw

        nc.sync.dma_start(wt_raw[:].bitcast(I32), wt_rows[:, 0:LAST, :].bitcast(I32))
        w1_raw = [load_w1(0)]
        nc.sync.dma_start(offsets[:], offs)
        nc.sync.dma_start(gain_rows[0:R_PASSES, :], gain.rearrange("(b c) -> b c", c=PASS))
        for q in range(QUADRANTS):
            nc.sync.dma_start(
                tab_raw_scales[32 * q + TAB_ROW : 32 * q + TAB_ROW + 4 * K_PASSES, :].bitcast(I32),
                tab_scales[:, 4 * q : 4 * q + 4, :].bitcast(I32),
            )
        w1_raw.append(load_w1(1))
        tab_raw = []
        for a in range(K_PASSES):
            raw = rows.tile([P, T], I32, name="tab_raw", tag="windows")
            nc.sync.dma_start(raw[:], tab_words[a].rearrange("p t i -> p (t i)").bitcast(I32))
            tab_raw.append(raw)
        for q in range(QUADRANTS):
            nc.sync.dma_start(
                wt_raw_scales[32 * q : 32 * q + 4, :, :].bitcast(I32),
                wt_scales[:, 4 * q : 4 * q + 4, :].rearrange("a r c -> r a c").bitcast(I32),
            )

        turned = psum.tile([P, PACK, P], F32, name="turned", tag="bank7")
        for t in range(PACK):
            nc.tensor.transpose(turned[:, t, :], gain_rows[:].rearrange("p (m t) -> p t m", t=PACK)[:, t, :], identity[:])
        nc.scalar.copy(gain_sb[:], turned[:, :, 0:R_PASSES])
        nc.scalar.activation(neg_gain[:], turned[:, :, 0:R_PASSES], ACT.Copy, scale=-1.0)

        wt_codes = {}

        def deal_wt(b, g, raw, copy):
            wt_codes[b, g] = keep.tile([P, 2 * PASS], U8, name="wt_codes%d_%d" % (b, g), align_bytes=64)
            copy(
                wt_codes[b, g][:].bitcast(U16).rearrange("p (t q) -> p t q", t=PACK),
                raw[:, 2 * PASS * g : 2 * PASS * (g + 1)].bitcast(U16).rearrange("p (q t) -> p t q", t=PACK),
            )

        wt_plane = keep.tile([P, R_PASSES, K], U8, name="wt_plane", align_bytes=64)
        for b in range(LAST):
            for g in range(K_PASSES):
                deal_wt(b, g, wt_raw[:, b, :], nc.vector.tensor_copy)

        w1_codes = keep.tile([P, K_PASSES, H], U32, name="w1_codes", align_bytes=64)
        w1_plane = keep.tile([P, K_PASSES, H], U8, name="w1_plane", align_bytes=64)
        v_codes = keep.tile([P, K_PASSES, S], U32, name="v_codes", align_bytes=64)
        v_plane = keep.tile([P, S], U8, name="v_plane", align_bytes=64)

        def round_w1(a, b, copy):
            grouped = stage.tile([P, PASS * PACK], BF16, name="grouped", tag="stage", align_bytes=64)
            copy(
                grouped[:].rearrange("p (t m j) -> p m t j", t=PACK, j=PACK),
                w1_raw[a][:, :, PASS * b : PASS * (b + 1)].rearrange("p j (m t) -> p m t j", t=PACK),
            )
            return grouped

        def quantise_w1(a, b, grouped):
            cols = slice(PASS * b, PASS * (b + 1))
            nc.vector.quantize_mx(w1_codes[:, a, cols].bitcast(FP8X4), w1_plane[:, a, cols], grouped[:])

        first = [round_w1(0, b, nc.scalar.copy if b == 0 else nc.vector.tensor_copy) for b in range(R_PASSES)]
        for b in (1, 2, 0):
            quantise_w1(0, b, first[b])
        nc.vector.tensor_copy(v_plane[:], tab_raw_scales[:].indirect(offsets[:]))
        second = [round_w1(1, b, nc.vector.tensor_copy if b == 0 else nc.scalar.copy) for b in range(R_PASSES)]
        quantise_w1(1, 0, second[0])
        for a in range(K_PASSES):
            nc.vector.tensor_copy(v_codes[:, a, :], tab_raw[a][:].bitcast(U32).indirect(offsets[:]))
            quantise_w1(1, a + 1, second[a + 1])

        for b in range(R_PASSES):
            nc.vector.tensor_copy(
                wt_plane[:, b, :].rearrange("p (g t q) -> p g t q", t=PACK, q=P),
                wt_raw_scales[:, b, :].rearrange("p (g q t) -> p g t q", t=PACK, q=P),
            )

        slope = [keep.tile([P, PACK, S], F32, name="slope%d" % b) for b in range(R_PASSES)]

        def first_product(b, t):
            cols = slice(PASS * b + P * t, PASS * b + P * (t + 1))
            acc = psum.tile([P, S], F32, name="acc", tag="bank%d" % t)
            for a in range(K_PASSES):
                nc.tensor.matmul_mx(
                    acc[:],
                    lhsT=w1_codes[:, a, cols].bitcast(FP8X4),
                    lhsT_scale=w1_plane[:, a, cols],
                    rhs=v_codes[:, a, :].bitcast(FP8X4),
                    rhs_scale=v_plane[TAB_ROW + 4 * a : P, :],
                    start=(a == 0),
                    stop=(a == K_PASSES - 1),
                )
            nc.scalar.activation(slope[b][:, t, :], acc[:], ACT.Tanh)

        def square(b, t):
            nc.scalar.activation(slope[b][:, t, :], slope[b][:, t, :], ACT.Square)

        def gain_times_one_minus(b, t):
            nc.scalar.activation(
                slope[b][:, t, :],
                slope[b][:, t, :],
                ACT.Identity,
                bias=gain_sb[:, t, b : b + 1],
                scale=neg_gain[:, t, b : b + 1],
            )

        for b in range(R_PASSES):
            for i in range(PACK + 2):
                if i < PACK:
                    first_product(b, i)
                if 1 <= i <= PACK:
                    square(b, i - 1)
                if i >= 2:
                    gain_times_one_minus(b, i - 2)

        banks = {}
        for h in range(2):
            for g in range(K_PASSES):
                for u in range(2):
                    banks[h, g, u] = psum.tile(
                        [P, 2, HALF], F32, name="y_acc", tag="bank%d" % (4 * (1 - h) + 2 * g + u)
                    )

        def g_rows(b):
            return gT[PASS * b : PASS * (b + 1), :].rearrange("(p t) c -> p t c", t=PACK)

        def slice_major(ap, run):
            return ap.rearrange("p t (c i) -> p c t i", i=run)

        def word_major(ap, run):
            return ap.rearrange("p (c i t) -> p c t i", i=run, t=PACK)

        def interleave(dst, src, copy):
            copy(word_major(dst, COPY_RUN), slice_major(src, COPY_RUN))

        def pick_and_scale(dst, window, t, c0, c1):
            nc.vector.tensor_tensor(
                dst, window[:].indirect(offsets[:, c0 // 16 : c1 // 16]), slope[LAST][:, t, c0:c1], ALU.mult
            )

        def second_product(b, h, d_codes, d_plane):
            for g in range(K_PASSES):
                for t in range(PACK):
                    n0 = PASS * g + P * t
                    nc.tensor.matmul_mx(
                        banks[h, g, t // 2][:, t % 2, :],
                        lhsT=wt_codes[b, g][:, 2 * P * t : 2 * P * (t + 1)].bitcast(FP4X4),
                        lhsT_scale=wt_plane[:, b, n0 : n0 + P],
                        rhs=d_codes.bitcast(FP8X4),
                        rhs_scale=d_plane,
                        start=(b == 0 and t % 2 == 0),
                        stop=(b == LAST and t % 2 == 1),
                    )

        for b in range(LAST):
            picked = keep.tile([P, PACK, S], F32, name="picked%d" % b)
            for t0, t1 in ((0, 2), (2, 3), (3, 4)) if b == LAST - 1 else ((0, 2), (2, 4)):
                windows = rows.tile([P, t1 - t0, T], F32, name="windows", tag="windows")
                nc.sync.dma_start(windows[:], g_rows(b)[:, t0:t1, :])
                for t in range(t0, t1):
                    nc.vector.tensor_copy(picked[:, t, :], windows[:, t - t0, :].indirect(offsets[:]))
            grouped = stage.tile([P, S * PACK], BF16, name="d_grouped", tag="stage", align_bytes=64)
            nc.vector.tensor_tensor(
                word_major(grouped[:], PRODUCT_RUN),
                slice_major(slope[b][:], PRODUCT_RUN),
                slice_major(picked[:], PRODUCT_RUN),
                ALU.mult,
            )
            d_codes = keep.tile([P, S], U32, name="d_codes%d" % b, align_bytes=64)
            d_plane = keep.tile([P, S], U8, name="d_plane%d" % b, align_bytes=64)
            nc.vector.quantize_mx(d_codes[:].bitcast(FP8X4), d_plane[:], grouped[:])
            for h in range(2):
                cols = slice(HALF * h, HALF * (h + 1))
                second_product(b, h, d_codes[:, cols], d_plane[:, cols])

        final = PACK - 1
        delta_a = keep.tile([P, PACK, HALF], F32, name="delta_a")
        delta_b = keep.tile([P, PACK + 1, HALF], F32, name="delta_b", align_bytes=64)
        for t in range(PACK):
            window = rows.tile([P, T], F32, name="window", tag="windows")
            nc.sync.dma_start(window[:], g_rows(LAST)[:, t, :])
            if t < final:
                pick_and_scale(delta_a[:, t, :], window, t, 0, HALF)
                pick_and_scale(delta_b[:, t, :], window, t, HALF, S)
        wt_late = rows.tile([P, 2 * K], U8, name="wt_late", tag="windows")
        nc.sync.dma_start(wt_late[:].bitcast(I32), wt_rows[:, LAST, :].bitcast(I32))
        for g in range(K_PASSES):
            deal_wt(LAST, g, wt_late, nc.scalar.copy)

        def last_half(h, delta, grouped):
            d_codes = keep.tile([P, HALF], U32, name="last_codes%d" % h, align_bytes=64)
            d_plane = keep.tile([P, HALF], U8, name="last_plane%d" % h, align_bytes=64)
            quarters = [slice(QUARTER * i, QUARTER * (i + 1)) for i in range(2)]
            for cols in quarters:
                pick_and_scale(delta[:, final, cols], window, final, HALF * h + cols.start, HALF * h + cols.stop)
            for i, cols in enumerate(quarters):
                interleave(grouped[i], delta[:, 0:PACK, cols], nc.vector.tensor_copy)
            for i, cols in enumerate(quarters):
                nc.vector.quantize_mx(d_codes[:, cols].bitcast(FP8X4), d_plane[:, cols], grouped[i])
            second_product(LAST, h, d_codes[:], d_plane[:])

        last_half(0, delta_a, [delta_b[:, final + 1, :].bitcast(BF16), delta_b[:, final, :].bitcast(BF16)])
        grouped = stage.tile([P, 2, QUARTER * PACK], BF16, name="d_grouped", tag="stage", align_bytes=64)
        last_half(1, delta_b, [grouped[:, 0, :], grouped[:, 1, :]])

        y_plane = keep.tile([P, K_PASSES, S], U8, name="y_plane", align_bytes=64)
        y_codes = [keep.tile([P, S], U32, name="y_codes%d" % g, align_bytes=64) for g in range(K_PASSES)]
        for h in range(2):
            cols = slice(HALF * h, HALF * (h + 1))
            y = big.tile([P, K_PASSES, PACK, HALF], F32, name="y", tag="big")
            y_grouped = []
            for g in range(K_PASSES):
                shared = h == 1 and g == K_PASSES - 1
                out_rows = out_0[PASS * g : PASS * (g + 1), cols].rearrange("(p t) m -> p t m", t=PACK)
                for u in range(2):
                    copy = nc.vector.tensor_copy if shared and u == 1 else nc.scalar.copy
                    copy(y[:, g, 2 * u : 2 * u + 2, :], banks[h, g, u][:])
                    nc.sync.dma_start(out_rows[:, 2 * u : 2 * u + 2, :], y[:, g, 2 * u : 2 * u + 2, :])
                tile = stage.tile([P, HALF * PACK], BF16, name="y_grouped", tag="stage", align_bytes=64)
                if shared:
                    interleave(tile[:, : QUARTER * PACK], y[:, g, :, :QUARTER], nc.scalar.copy)
                    interleave(tile[:, QUARTER * PACK :], y[:, g, :, QUARTER:], nc.vector.tensor_copy)
                else:
                    interleave(tile[:], y[:, g, :, :], nc.vector.tensor_copy)
                y_grouped.append(tile)
            for g in range(K_PASSES):
                nc.vector.quantize_mx(y_codes[g][:, cols].bitcast(FP8X4), y_plane[:, g, cols], y_grouped[g][:])
                if h == 1:
                    nc.sync.dma_start(out_1[g].rearrange("p m t -> p (m t)").bitcast(I32), y_codes[g][:].bitcast(I32))
        for q in range(QUADRANTS):
            nc.sync.dma_start(
                out_2[:, 4 * q : 4 * q + 4, :].rearrange("g r m -> r g m").bitcast(I32),
                y_plane[32 * q : 32 * q + 4, :, :].bitcast(I32),
            )
